import numpy as np
import ml_dtypes


def mxq(x, axis, fmt="e4m3"):
    dtype, down = {"e4m3": (ml_dtypes.float8_e4m3fn, 7), "e5m2": (ml_dtypes.float8_e5m2, 14)}[fmt]
    v = np.moveaxis(np.asarray(x, np.float32).astype(ml_dtypes.bfloat16).astype(np.float64), axis, -1)
    blocks = v.reshape(v.shape[:-1] + (-1, 32))
    amax = np.abs(blocks).max(-1, keepdims=True)
    byte = np.maximum(np.where(amax > 0, np.frexp(amax)[1] - 1 + 127, 0) - down, 1)
    scale = np.exp2(byte - 127.0)
    codes = (blocks / scale).astype(np.float32).astype(dtype).astype(np.float64)
    return np.moveaxis((codes * scale).reshape(v.shape), -1, axis)


WIDE = False


def mx_kscale(k):
    if not WIDE:
        return np.ones(k)
    levels = np.array([10, -10, 5, -5, 0])
    if k % 512:
        return np.exp2(np.random.permutation(np.resize(levels, k // 32))).repeat(32)
    a = np.empty((k // 512, 16))
    for p in range(k // 512):
        a[p, :8] = np.random.permutation(np.resize(levels, 8))
        for g in range(8):
            far = levels[np.abs(levels - a[p, g]) >= 10]
            a[p, g + 8] = far[np.random.randint(len(far))]
    return np.exp2(a.ravel()).repeat(32)


BF16 = ml_dtypes.bfloat16


def bf(x):
    return np.asarray(x, np.float32).astype(BF16)


def f64(x):
    return np.asarray(x).astype(np.float64)


E2M1 = np.array([0.0, 0.5, 1.0, 1.5, 2.0, 3.0, 4.0, 6.0, -0.0, -0.5, -1.0, -1.5, -2.0, -3.0, -4.0, -6.0])


def pack_weight(w, fmt):
    k, n = w.shape
    w = f64(bf(w)).reshape(k // 32, 32, n)
    amax = np.abs(w).max(1)
    if fmt == "e4m3":
        byte = np.frexp(amax)[1] - 1 + 127 - 7
    else:
        mant, ex = np.frexp(amax / 6.0)
        byte = np.where(mant > 0.5, ex, ex - 1) + 127
    byte = np.clip(np.where(amax > 0, byte, 1), 1, 254)
    scaled = (w * np.exp2(127.0 - byte)[:, None, :]).reshape(k, n).astype(np.float32)
    by_word = np.ascontiguousarray(scaled.reshape(k // 512, 128, 4, n).transpose(0, 1, 3, 2))
    if fmt == "e4m3":
        words = by_word.astype(ml_dtypes.float8_e4m3fn).view(np.uint8)
    else:
        c = by_word.astype(ml_dtypes.float4_e2m1fn).view(np.uint8) & 0xF
        words = c[..., 0::2] | (c[..., 1::2] << 4)
    return np.ascontiguousarray(words), np.ascontiguousarray(byte.astype(np.uint8).reshape(k // 512, 16, n))


def unpack_weight(words, scales, fmt):
    g, p, n, _ = words.shape
    if fmt == "e4m3":
        vals = np.ascontiguousarray(words).view(ml_dtypes.float8_e4m3fn).astype(np.float64)
    else:
        nib = np.empty((g, p, n, 4), np.uint8)
        nib[..., 0::2] = words & 0xF
        nib[..., 1::2] = words >> 4
        vals = E2M1[nib]
    vals = vals * np.repeat(np.exp2(scales.astype(np.float64) - 127.0), 8, axis=1)[..., None]
    return vals.transpose(0, 1, 3, 2).reshape(g * 512, n)
def pack4(w):
    words, scales = pack_weight(w, "e2m1")
    return words.reshape(words.shape[0], 128, -1), scales


def unpack4(words, scales):
    return unpack_weight(words.reshape(words.shape[0], 128, -1, 2), scales, "e2m1")


def planes(Y):
    n, m = Y.shape
    b = f64(bf(Y)).reshape(n // 32, 32, m)
    amax = np.abs(b).max(1)
    byte = np.clip(np.where(amax > 0, np.frexp(amax)[1] - 1 + 127 - 7, 1), 1, 254)
    codes = (b * np.exp2(127.0 - byte)[:, None, :]).reshape(n, m).astype(np.float32).astype(ml_dtypes.float8_e4m3fn).view(np.uint8)
    words = codes.reshape(n // 512, 128, 4, m).transpose(0, 1, 3, 2)
    return np.ascontiguousarray(words), np.ascontiguousarray(byte.astype(np.uint8).reshape(n // 512, 16, m))


D, T, N = 1024, 1536, 512
ALPHA = 0.75

def model(base, g):
    s, t = mx_kscale(T), mx_kscale(D)
    x = np.random.randn(T, D) * g
    w = 0.5 * np.exp(0.3 * np.random.randn(T)) / np.sqrt(T)
    u_words, u_scales = pack4(x * s[:, None])
    v_words, v_scales = pack4(x * (w / s)[:, None] * t)
    a = bf((base + 0.5 * np.random.randn(D, N) / np.sqrt(D)) / t[:, None])
    return u_words, u_scales, v_words, v_scales, a

def setup_inputs():
    g = np.exp(0.4 * np.random.randn(D))
    base = np.random.randn(D, N) / np.sqrt(D)
    u1w, u1s, v1w, v1s, a1 = model(base, g)
    u2w, u2s, v2w, v2s, a2 = model(base, g)
    lam = 0.15 * np.sqrt(T) * g ** 2 * np.exp(0.2 * np.random.randn(D))
    return {"u1_words": u1w, "u1_scales": u1s, "v1_words": v1w, "v1_scales": v1s,
            "u2_words": u2w, "u2_scales": u2s, "v2_words": v2w, "v2_scales": v2s,
            "a1": a1, "a2": a2, "base": bf(base), "lam": bf(lam)}

def reference(u1_words, u1_scales, v1_words, v1_scales, u2_words, u2_scales, v2_words, v2_scales, a1, a2, base, lam):
    shrink = ALPHA + (1.0 - ALPHA) * np.eye(D)
    H1 = (unpack4(u1_words, u1_scales).T @ unpack4(v1_words, v1_scales)) * shrink
    H2 = (unpack4(u2_words, u2_scales).T @ unpack4(v2_words, v2_scales)) * shrink
    P1 = mxq(H1, 1, "e4m3") @ mxq(f64(a1), 0, "e4m3")
    P2 = mxq(H2, 1, "e4m3") @ mxq(f64(a2), 0, "e4m3")
    y = P1 + P2 + f64(lam)[:, None] * f64(base)
    Y = y
    words, scales = planes(Y)
    return y, words, scales

@@ -1,0 +1,266 @@
+from contextlib import ExitStack
+
+import concourse.mybir as mybir
+from concourse.masks import make_identity
+
+D, T, N = 1024, 1536, 512
+ALPHA = 0.75
+FLOPS = 2 * (2 * D * D * T + 2 * D * D * N)
+
+F32 = mybir.dt.float32
+BF16 = mybir.dt.bfloat16
+I32 = mybir.dt.int32
+U32 = mybir.dt.uint32
+U8 = mybir.dt.uint8
+FP8X4 = mybir.dt.float8_e4m3fn_x4
+FP4X4 = mybir.dt.float4_e2m1fn_x4
+ACT = mybir.ActivationFunctionType
+ALU = mybir.AluOpType
+
+P = 128
+PACK = 4
+GROUP = P * PACK
+TOKEN_PASSES = T // GROUP
+SLOTS_PER_BANK = 4
+COLS = GROUP // SLOTS_PER_BANK
+HALF_N = N // 2
+SCALAR_COLS = 80
+
+
+def tile_regmean_merge_rhs_k5_kernel(
+    tc, u1_words, u1_scales, v1_words, v1_scales, u2_words, u2_scales, v2_words, v2_scales,
+    a1, a2, base, lam, out_0, out_1, out_2,
+):
+    nc = tc.nc
+    u_words, v_words = (u1_words, u2_words), (v1_words, v2_words)
+    weights = (a1, a2)
+
+    with ExitStack() as ctx:
+        keep = ctx.enter_context(tc.tile_pool(name="keep", bufs=1))
+        ring = ctx.enter_context(tc.tile_pool(name="ring", bufs=3))
+        psum = ctx.enter_context(tc.psum_pool(name="psum", bufs=8))
+        ctx.enter_context(tc.manual_schedule())
+
+        def new(name, shape, dtype):
+            return keep.tile(shape, dtype, name=name, align_bytes=64)
+
+        def load_codes(name, words, half):
+            codes = new(name, [P, TOKEN_PASSES, 2 * GROUP], U8)
+            src = words.rearrange("g p n -> p g n")[:, :, 2 * GROUP * half : 2 * GROUP * (half + 1)]
+            nc.sync.dma_start(out=codes[:].bitcast(I32), in_=src.bitcast(I32))
+            return codes
+
+        def cleared_plane(name, width):
+            plane = new(name, [P, TOKEN_PASSES, width], U8)
+            nc.vector.memset(plane[:].bitcast(I32), 0)
+            return plane
+
+        def load_scale_rows(queue, plane, scales, col0, rows):
+            width = plane.shape[2]
+            for r in rows:
+                src = scales.rearrange("g (q r) n -> r q g n", r=4)[r][:, :, col0 : col0 + width]
+                queue.dma_start(out=plane[r:P:32, :, :].bitcast(I32), in_=src.bitcast(I32))
+
+        def sort_v(name, codes, plane):
+            s_codes = new(name + "_codes", [P, PACK, TOKEN_PASSES, 2 * P], U8)
+            s_plane = new(name + "_plane", [P, PACK, TOKEN_PASSES, P], U8)
+            nc.vector.tensor_copy(
+                out=s_codes[:].rearrange("p t g n -> p t (g n)").bitcast(I32).rearrange("p t (x a e) -> p x t a e", a=2, e=2),
+                in_=codes[:].rearrange("p g n -> p (g n)").bitcast(I32).rearrange("p (x a t e) -> p x t a e", a=2, t=4, e=2),
+            )
+            nc.vector.tensor_copy(
+                out=s_plane[:].bitcast(I32).rearrange("p t g (x w) -> p x g t w", w=4),
+                in_=plane.bitcast(I32).rearrange("p g (x w t) -> p x g t w", w=4, t=4),
+            )
+            return s_codes, s_plane
+
+        def load_weight(m, g):
+            raw = new("a_raw%d%d" % (m, g), [P, PACK, N], BF16)
+            src = weights[m][GROUP * g : GROUP * (g + 1), :].rearrange("(x t b) n -> b x t n", t=4, b=4)
+            for b in range(4):
+                nc.sync.dma_start(out=raw[b:P:4, :, :], in_=src[b])
+            return raw
+
+        def interleave(copy, dst, src):
+            copy(
+                out=dst.rearrange("p (c i) t -> p c t i", i=4),
+                in_=src.rearrange("p t (c i) -> p c t i", i=4),
+            )
+
+        def quantise(name, src, width):
+            codes = new(name + "_codes", [P, width], U32)
+            plane = new(name + "_plane", [P, width], U8)
+            nc.vector.quantize_mx(out=codes[:].bitcast(FP8X4), scales=plane[:], in_=src)
+            return codes, plane
+
+        v1_plane = {1: cleared_plane("v1_plane1", GROUP)}
+        u1_plane = {0: cleared_plane("u1_plane0", GROUP)}
+        v_raw = {(0, 1): load_codes("v_raw01", v_words[0], 1)}
+        u_codes = {(0, 0): load_codes("u_codes00", u_words[0], 0)}
+        load_scale_rows(nc.sync, v1_plane[1], v1_scales, GROUP, range(4))
+        load_scale_rows(nc.sync, u1_plane[0], u1_scales, 0, range(2))
+        load_scale_rows(nc.gpsimd, u1_plane[0], u1_scales, 0, range(2, 4))
+        ident = new("ident", [P, P], BF16)
+        make_identity(nc, ident[:])
+
+        v1_plane[0] = cleared_plane("v1_plane0", GROUP)
+        v2_plane = cleared_plane("v2_plane", D)
+        u2_plane = cleared_plane("u2_plane", D)
+        u1_plane[1] = cleared_plane("u1_plane1", GROUP)
+        shrink = new("shrink", [P, PACK, P, PACK], BF16)
+        nc.vector.memset(shrink[:], ALPHA)
+        nc.scalar.activation(
+            out=shrink[:].rearrange("p i (h l) t -> p i h (l t)", l=4)[:, :, :, 0:16:5],
+            in_=ident[:].rearrange("p (h i) -> p i h", i=4).unsqueeze(3).to_broadcast([P, 4, 32, 4]),
+            func=ACT.Copy, scale=1.0 - ALPHA, bias=ALPHA,
+        )
+        load_scale_rows(nc.gpsimd, v2_plane, v2_scales, 0, range(4))
+        load_scale_rows(nc.gpsimd, u2_plane, u2_scales, 0, range(4))
+
+        load_scale_rows(nc.sync, v1_plane[0], v1_scales, 0, range(4))
+        v_raw[0, 0] = load_codes("v_raw00", v_words[0], 0)
+        v_raw[1, 1] = load_codes("v_raw11", v_words[1], 1)
+        u_codes[1, 0] = load_codes("u_codes10", u_words[1], 0)
+        v_raw[1, 0] = load_codes("v_raw10", v_words[1], 0)
+        a_raw = {(m, g): load_weight(m, g) for m in range(2) for g in (1, 0)}
+        u_codes[0, 1] = load_codes("u_codes01", u_words[0], 1)
+        load_scale_rows(nc.sync, u1_plane[1], u1_scales, GROUP, range(4))
+        lam_sb = new("lam_sb", [P, 2, PACK], BF16)
+        nc.sync.dma_start(out=lam_sb[:], in_=lam.rearrange("(g p t) -> p g t", g=2, t=PACK))
+        base_sb = []
+        for g in range(2):
+            base_g = new("base%d" % g, [P, PACK, N], BF16)
+            nc.sync.dma_start(out=base_g[:], in_=base[GROUP * g : GROUP * (g + 1), :].rearrange("(p t) n -> p t n", t=PACK))
+            base_sb.append(base_g)
+        u_codes[1, 1] = load_codes("u_codes11", u_words[1], 1)
+
+        def half_of(plane, half):
+            return plane[:, :, GROUP * half : GROUP * (half + 1)]
+
+        u_plane = {(0, 0): u1_plane[0][:], (0, 1): u1_plane[1][:], (1, 0): half_of(u2_plane, 0), (1, 1): half_of(u2_plane, 1)}
+        v_plane = {(0, 0): v1_plane[0][:], (0, 1): v1_plane[1][:], (1, 0): half_of(v2_plane, 0), (1, 1): half_of(v2_plane, 1)}
+
+        v_sorted, a_mixed, a_mx, h_bf, h_mx, y_f32, y_bf = {}, {}, {}, {}, {}, {}, {}
+        y_plane = [new("y_plane%d" % g, [P, N], U8) for g in range(2)]
+
+        def do_sort_v(m, gj):
+            v_sorted[m, gj] = sort_v("v%d%d" % (m, gj), v_raw[m, gj], v_plane[m, gj])
+
+        def do_mix_a(copy, m, g, half):
+            if half == 0:
+                a_mixed[m, g] = new("a_mixed%d%d" % (m, g), [P, N, PACK], BF16)
+            cols = slice(HALF_N * half, HALF_N * (half + 1))
+            interleave(copy, a_mixed[m, g][:, cols, :], a_raw[m, g][:, :, cols])
+
+        def do_quant_a(m, g):
+            a_mx[m, g] = quantise("a%d%d" % (m, g), a_mixed[m, g][:].rearrange("p n t -> p (n t)"), N)
+
+        def do_quant_h(gi, m, gj):
+            h_mx[gi, m, gj] = quantise("h%d%d%d" % (gi, m, gj), h_bf[gi, m, gj][:].rearrange("p i x t -> p (i x t)"), GROUP)
+
+        def gram_bank(gi, m, gj, unit):
+            if unit == 0:
+                h_tile = ring.tile([P, PACK, P, PACK], BF16, name="h_tile", align_bytes=64)
+                h_bf[gi, m, gj] = h_tile
+            chunk, first = divmod(unit * SLOTS_PER_BANK, PACK)
+            s_codes, s_plane = v_sorted[m, gj]
+            bank = psum.tile([P, GROUP], F32, name="bank")
+            for k in range(SLOTS_PER_BANK):
+                for g in range(TOKEN_PASSES):
+                    nc.tensor.matmul_mx(
+                        out=bank[:, COLS * k : COLS * (k + 1)],
+                        lhsT=s_codes[:, first + k, g, :].bitcast(FP4X4),
+                        lhsT_scale=s_plane[:, first + k, g, :],
+                        rhs=u_codes[m, gi][:, g, 2 * COLS * chunk : 2 * COLS * (chunk + 1)].bitcast(FP4X4),
+                        rhs_scale=u_plane[m, gi][:, g, COLS * chunk : COLS * (chunk + 1)],
+                        start=(g == 0), stop=(g == TOKEN_PASSES - 1),
+                    )
+            xs = slice(COLS // PACK * chunk, COLS // PACK * (chunk + 1))
+            ts = slice(first, first + SLOTS_PER_BANK)
+            sums = bank[:].rearrange("p (t x i) -> p i x t", t=SLOTS_PER_BANK, i=PACK)
+            dst = h_bf[gi, m, gj][:, :, xs, ts]
+            if gi == gj:
+                nc.vector.tensor_tensor(out=dst, in0=sums, in1=shrink[:, :, xs, ts], op=ALU.mult)
+            else:
+                nc.scalar.activation(out=dst, in_=sums, func=ACT.Copy, scale=ALPHA)
+
+        def result_bank(gi, half, t):
+            cols = slice(HALF_N * half, HALF_N * (half + 1))
+            if t == 0:
+                y_f32[gi, half] = new("y_f32%d%d" % (gi, half), [P, PACK, HALF_N], F32)
+            bank = psum.tile([P, GROUP], F32, name="bank")
+            terms = [(m, gj) for m in range(2) for gj in (1, 0)]
+            for k, (m, gj) in enumerate(terms):
+                h_codes, h_plane = h_mx[gi, m, gj]
+                a_codes, a_plane = a_mx[m, gj]
+                nc.tensor.matmul_mx(
+                    out=bank[:, :HALF_N],
+                    lhsT=h_codes[:, P * t : P * (t + 1)].bitcast(FP8X4), lhsT_scale=h_plane[:, P * t : P * (t + 1)],
+                    rhs=a_codes[:, cols].bitcast(FP8X4), rhs_scale=a_plane[:, cols],
+                    start=(k == 0), stop=(k == len(terms) - 1),
+                )
+            y = y_f32[gi, half]
+            nc.vector.scalar_tensor_tensor(
+                out=y[:, t, :], in0=base_sb[gi][:, t, cols], scalar=lam_sb[:, gi, t : t + 1], in1=bank[:, :HALF_N],
+                op0=ALU.mult, op1=ALU.add,
+            )
+            if t % 2 == 1:
+                rows = out_0[GROUP * gi : GROUP * (gi + 1), cols].rearrange("(p t) n -> p t n", t=PACK)
+                nc.sync.dma_start(out=rows[:, t - 1 : t + 1, :], in_=y[:, t - 1 : t + 1, :])
+
+        def do_mix_y(gi, half, scalar_cols):
+            y_tile = new("y_bf%d%d" % (gi, half), [P, HALF_N, PACK], BF16)
+            y_bf[gi, half] = y_tile
+            y = y_f32[gi, half]
+            interleave(nc.scalar.copy, y_tile[:, :scalar_cols, :], y[:, :, :scalar_cols])
+            if scalar_cols < HALF_N:
+                interleave(nc.vector.tensor_copy, y_tile[:, scalar_cols:, :], y[:, :, scalar_cols:])
+
+        def do_quant_y(gi, half):
+            cols = slice(HALF_N * half, HALF_N * (half + 1))
+            codes = new("y_codes%d%d" % (gi, half), [P, HALF_N], U32)
+            nc.vector.quantize_mx(
+                out=codes[:].bitcast(FP8X4), scales=y_plane[gi][:, cols], in_=y_bf[gi, half][:].rearrange("p n t -> p (n t)")
+            )
+            words = out_1[gi].rearrange("p n t -> p (n t)").bitcast(I32)
+            nc.sync.dma_start(out=words[:, cols], in_=codes[:].bitcast(I32))
+            if half == 1:
+                rows = out_2[gi].rearrange("(q r) n -> r q n", r=4)
+                for r in range(4):
+                    queue = nc.scalar if r % 2 else nc.sync
+                    queue.dma_start(out=rows[r].bitcast(I32), in_=y_plane[gi][r:P:32, :].bitcast(I32))
+
+        def gram(gi, m, gj, after):
+            for unit in range(4):
+                gram_bank(gi, m, gj, unit)
+                for job in after.get(unit, []):
+                    job()
+
+        def result(gi, half, after):
+            for t in range(PACK):
+                result_bank(gi, half, t)
+                for job in after.get(t, []):
+                    job()
+
+        s_copy, v_copy = nc.scalar.copy, nc.vector.tensor_copy
+        do_sort_v(0, 1)
+        gram(0, 0, 1, {0: [lambda: do_sort_v(0, 0)]})
+        gram(0, 0, 0, {
+            0: [lambda: do_quant_h(0, 0, 1), lambda: do_mix_a(s_copy, 0, 1, 0), lambda: do_mix_a(s_copy, 0, 1, 1)],
+            1: [lambda: do_sort_v(1, 1), lambda: do_mix_a(s_copy, 0, 0, 0)],
+        })
+        gram(0, 1, 1, {
+            0: [lambda: do_sort_v(1, 0), lambda: do_quant_h(0, 0, 0), lambda: do_mix_a(s_copy, 0, 0, 1)],
+            1: [lambda: do_quant_a(0, 1), lambda: do_mix_a(v_copy, 1, 1, 0), lambda: do_mix_a(v_copy, 1, 1, 1)],
+            2: [lambda: do_quant_a(0, 0)],
+            3: [lambda: do_mix_a(s_copy, 1, 0, 0), lambda: do_mix_a(s_copy, 1, 0, 1)],
+        })
+        gram(0, 1, 0, {0: [lambda: do_quant_h(0, 1, 1)], 1: [lambda: do_quant_a(1, 1)], 3: [lambda: do_quant_a(1, 0)]})
+        gram(1, 0, 1, {0: [lambda: do_quant_h(0, 1, 0)]})
+        result(0, 0, {0: [lambda: do_quant_h(1, 0, 1)]})
+        gram(1, 0, 0, {0: [lambda: do_mix_y(0, 0, HALF_N), lambda: do_quant_y(0, 0)]})
+        gram(1, 1, 1, {0: [lambda: do_quant_h(1, 0, 0)]})
+        gram(1, 1, 0, {0: [lambda: do_quant_h(1, 1, 1)]})
+        result(0, 1, {0: [lambda: do_quant_h(1, 1, 0)], 3: [lambda: do_mix_y(0, 1, HALF_N)]})
+        result(1, 0, {1: [lambda: do_quant_y(0, 1)], 3: [lambda: do_mix_y(1, 0, HALF_N)]})
+        result(1, 1, {1: [lambda: do_quant_y(1, 0)], 3: [lambda: do_mix_y(1, 1, SCALAR_COLS), lambda: do_quant_y(1, 1)]})

@@ -21,7 +21,7 @@ P = 128
 PACK = 4
 GROUP = P * PACK
 TOKEN_PASSES = T // GROUP
-SLOTS_PER_BANK = 4
+SLOTS_PER_BANK = 2
 COLS = GROUP // SLOTS_PER_BANK
 HALF_N = N // 2
 SCALAR_COLS = 80
@@ -108,17 +108,19 @@ def tile_regmean_merge_rhs_k5_kernel(
         u2_plane = cleared_plane("u2_plane", D)
         u1_plane[1] = cleared_plane("u1_plane1", GROUP)
         shrink = new("shrink", [P, PACK, P, PACK], BF16)
-        nc.vector.memset(shrink[:], ALPHA)
-        nc.scalar.activation(
-            out=shrink[:].rearrange("p i (h l) t -> p i h (l t)", l=4)[:, :, :, 0:16:5],
-            in_=ident[:].rearrange("p (h i) -> p i h", i=4).unsqueeze(3).to_broadcast([P, 4, 32, 4]),
-            func=ACT.Copy, scale=1.0 - ALPHA, bias=ALPHA,
-        )
-        load_scale_rows(nc.gpsimd, v2_plane, v2_scales, 0, range(4))
-        load_scale_rows(nc.gpsimd, u2_plane, u2_scales, 0, range(4))
 
-        load_scale_rows(nc.sync, v1_plane[0], v1_scales, 0, range(4))
+        def make_shrink():
+            nc.vector.memset(shrink[:], ALPHA)
+            nc.scalar.activation(
+                out=shrink[:].rearrange("p i (h l) t -> p i h (l t)", l=4)[:, :, :, 0:16:5],
+                in_=ident[:].rearrange("p (h i) -> p i h", i=4).unsqueeze(3).to_broadcast([P, 4, 32, 4]),
+                func=ACT.Copy, scale=1.0 - ALPHA, bias=ALPHA,
+            )
+
         v_raw[0, 0] = load_codes("v_raw00", v_words[0], 0)
+        load_scale_rows(nc.sync, v1_plane[0], v1_scales, 0, range(4))
+        load_scale_rows(nc.sync, v2_plane, v2_scales, 0, range(4))
+        load_scale_rows(nc.sync, u2_plane, u2_scales, 0, range(4))
         v_raw[1, 1] = load_codes("v_raw11", v_words[1], 1)
         u_codes[1, 0] = load_codes("u_codes10", u_words[1], 0)
         v_raw[1, 0] = load_codes("v_raw10", v_words[1], 0)
@@ -244,22 +246,21 @@ def tile_regmean_merge_rhs_k5_kernel(
 
         s_copy, v_copy = nc.scalar.copy, nc.vector.tensor_copy
         do_sort_v(0, 1)
+        make_shrink()
         gram(0, 0, 1, {0: [lambda: do_sort_v(0, 0)]})
-        gram(0, 0, 0, {
-            0: [lambda: do_quant_h(0, 0, 1), lambda: do_mix_a(s_copy, 0, 1, 0), lambda: do_mix_a(s_copy, 0, 1, 1)],
-            1: [lambda: do_sort_v(1, 1), lambda: do_mix_a(s_copy, 0, 0, 0)],
-        })
+        gram(0, 0, 0, {0: [lambda: do_quant_h(0, 0, 1)], 1: [lambda: do_sort_v(1, 1)]})
         gram(0, 1, 1, {
-            0: [lambda: do_sort_v(1, 0), lambda: do_quant_h(0, 0, 0), lambda: do_mix_a(s_copy, 0, 0, 1)],
-            1: [lambda: do_quant_a(0, 1), lambda: do_mix_a(v_copy, 1, 1, 0), lambda: do_mix_a(v_copy, 1, 1, 1)],
-            2: [lambda: do_quant_a(0, 0)],
-            3: [lambda: do_mix_a(s_copy, 1, 0, 0), lambda: do_mix_a(s_copy, 1, 0, 1)],
+            0: [lambda: do_sort_v(1, 0), lambda: do_quant_h(0, 0, 0), lambda: do_mix_a(s_copy, 0, 1, 0)],
+            1: [lambda: do_mix_a(s_copy, 0, 1, 1)],
+            2: [lambda: do_mix_a(v_copy, 0, 0, 0), lambda: do_mix_a(v_copy, 0, 0, 1)],
+            3: [lambda: do_mix_a(s_copy, 1, 1, 0), lambda: do_mix_a(s_copy, 1, 1, 1),
+                lambda: do_mix_a(s_copy, 1, 0, 0), lambda: do_mix_a(s_copy, 1, 0, 1)],
         })
-        gram(0, 1, 0, {0: [lambda: do_quant_h(0, 1, 1)], 1: [lambda: do_quant_a(1, 1)], 3: [lambda: do_quant_a(1, 0)]})
-        gram(1, 0, 1, {0: [lambda: do_quant_h(0, 1, 0)]})
-        result(0, 0, {0: [lambda: do_quant_h(1, 0, 1)]})
-        gram(1, 0, 0, {0: [lambda: do_mix_y(0, 0, HALF_N), lambda: do_quant_y(0, 0)]})
-        gram(1, 1, 1, {0: [lambda: do_quant_h(1, 0, 0)]})
+        gram(0, 1, 0, {0: [lambda: do_quant_h(0, 1, 1)], 1: [lambda: do_quant_a(0, 1)], 2: [lambda: do_quant_a(0, 0)]})
+        gram(1, 0, 1, {0: [lambda: do_quant_h(0, 1, 0)], 2: [lambda: do_quant_a(1, 1)]})
+        gram(1, 0, 0, {0: [lambda: do_quant_a(1, 0), lambda: do_quant_h(1, 0, 1)]})
+        result(0, 0, {0: [lambda: do_quant_h(1, 0, 0)], 3: [lambda: do_mix_y(0, 0, HALF_N)]})
+        gram(1, 1, 1, {1: [lambda: do_quant_y(0, 0)]})
         gram(1, 1, 0, {0: [lambda: do_quant_h(1, 1, 1)]})
         result(0, 1, {0: [lambda: do_quant_h(1, 1, 0)], 3: [lambda: do_mix_y(0, 1, HALF_N)]})
         result(1, 0, {1: [lambda: do_quant_y(0, 1)], 3: [lambda: do_mix_y(1, 0, HALF_N)]})

@@ -21,10 +21,9 @@ P = 128
 PACK = 4
 GROUP = P * PACK
 TOKEN_PASSES = T // GROUP
-SLOTS_PER_BANK = 2
-COLS = GROUP // SLOTS_PER_BANK
 HALF_N = N // 2
-SCALAR_COLS = 80
+COLS = 256
+SCALAR_COLS = 32
 
 
 def tile_regmean_merge_rhs_k5_kernel(
@@ -50,9 +49,9 @@ def tile_regmean_merge_rhs_k5_kernel(
             nc.sync.dma_start(out=codes[:].bitcast(I32), in_=src.bitcast(I32))
             return codes
 
-        def cleared_plane(name, width):
+        def cleared_plane(name, width, engine=nc.vector):
             plane = new(name, [P, TOKEN_PASSES, width], U8)
-            nc.vector.memset(plane[:].bitcast(I32), 0)
+            engine.memset(plane[:].bitcast(I32), 0)
             return plane
 
         def load_scale_rows(queue, plane, scales, col0, rows):
@@ -93,13 +92,12 @@ def tile_regmean_merge_rhs_k5_kernel(
             nc.vector.quantize_mx(out=codes[:].bitcast(FP8X4), scales=plane[:], in_=src)
             return codes, plane
 
-        v1_plane = {1: cleared_plane("v1_plane1", GROUP)}
+        v1_plane = {1: cleared_plane("v1_plane1", GROUP, nc.gpsimd)}
         u1_plane = {0: cleared_plane("u1_plane0", GROUP)}
+        load_scale_rows(nc.scalar, v1_plane[1], v1_scales, GROUP, range(4))
         v_raw = {(0, 1): load_codes("v_raw01", v_words[0], 1)}
         u_codes = {(0, 0): load_codes("u_codes00", u_words[0], 0)}
-        load_scale_rows(nc.sync, v1_plane[1], v1_scales, GROUP, range(4))
-        load_scale_rows(nc.sync, u1_plane[0], u1_scales, 0, range(2))
-        load_scale_rows(nc.gpsimd, u1_plane[0], u1_scales, 0, range(2, 4))
+        load_scale_rows(nc.sync, u1_plane[0], u1_scales, 0, range(4))
         ident = new("ident", [P, P], BF16)
         make_identity(nc, ident[:])
 
@@ -107,15 +105,16 @@ def tile_regmean_merge_rhs_k5_kernel(
         v2_plane = cleared_plane("v2_plane", D)
         u2_plane = cleared_plane("u2_plane", D)
         u1_plane[1] = cleared_plane("u1_plane1", GROUP)
-        shrink = new("shrink", [P, PACK, P, PACK], BF16)
+        shrink = new("shrink", [P, 32, 8, 2], BF16)
 
         def make_shrink():
             nc.vector.memset(shrink[:], ALPHA)
-            nc.scalar.activation(
-                out=shrink[:].rearrange("p i (h l) t -> p i h (l t)", l=4)[:, :, :, 0:16:5],
-                in_=ident[:].rearrange("p (h i) -> p i h", i=4).unsqueeze(3).to_broadcast([P, 4, 32, 4]),
-                func=ACT.Copy, scale=1.0 - ALPHA, bias=ALPHA,
-            )
+            for l in range(2):
+                nc.scalar.activation(
+                    out=shrink[:, :, PACK * l : PACK * (l + 1), l],
+                    in_=ident[:].rearrange("p (h i) -> p h i", i=PACK),
+                    func=ACT.Copy, scale=1.0 - ALPHA, bias=ALPHA,
+                )
 
         v_raw[0, 0] = load_codes("v_raw00", v_words[0], 0)
         load_scale_rows(nc.sync, v1_plane[0], v1_scales, 0, range(4))
@@ -142,16 +141,17 @@ def tile_regmean_merge_rhs_k5_kernel(
         u_plane = {(0, 0): u1_plane[0][:], (0, 1): u1_plane[1][:], (1, 0): half_of(u2_plane, 0), (1, 1): half_of(u2_plane, 1)}
         v_plane = {(0, 0): v1_plane[0][:], (0, 1): v1_plane[1][:], (1, 0): half_of(v2_plane, 0), (1, 1): half_of(v2_plane, 1)}
 
-        v_sorted, a_mixed, a_mx, h_bf, h_mx, y_f32, y_bf = {}, {}, {}, {}, {}, {}, {}
+        v_sorted, a_mixed, a_mx, h_bf, h_mx, y_f32, y_bf, h_pairs = {}, {}, {}, {}, {}, {}, {}, {}
+        y_codes = [new("y_codes%d" % g, [P, N], U32) for g in range(2)]
         y_plane = [new("y_plane%d" % g, [P, N], U8) for g in range(2)]
 
         def do_sort_v(m, gj):
             v_sorted[m, gj] = sort_v("v%d%d" % (m, gj), v_raw[m, gj], v_plane[m, gj])
 
-        def do_mix_a(copy, m, g, half):
+        def do_mix_a(copy, m, g, half, parts=2):
             if half == 0:
                 a_mixed[m, g] = new("a_mixed%d%d" % (m, g), [P, N, PACK], BF16)
-            cols = slice(HALF_N * half, HALF_N * (half + 1))
+            cols = slice(N // parts * half, N // parts * (half + 1))
             interleave(copy, a_mixed[m, g][:, cols, :], a_raw[m, g][:, :, cols])
 
         def do_quant_a(m, g):
@@ -161,75 +161,91 @@ def tile_regmean_merge_rhs_k5_kernel(
             h_mx[gi, m, gj] = quantise("h%d%d%d" % (gi, m, gj), h_bf[gi, m, gj][:].rearrange("p i x t -> p (i x t)"), GROUP)
 
         def gram_bank(gi, m, gj, unit):
+            chunk, pair = divmod(unit, 2)
             if unit == 0:
                 h_tile = ring.tile([P, PACK, P, PACK], BF16, name="h_tile", align_bytes=64)
                 h_bf[gi, m, gj] = h_tile
-            chunk, first = divmod(unit * SLOTS_PER_BANK, PACK)
+            if pair == 0:
+                h_stage = ring.tile([P, 2, COLS, 2], BF16, name="h_stage", align_bytes=64, bufs=4)
+                h_pairs[gi, m, gj, chunk] = h_stage
             s_codes, s_plane = v_sorted[m, gj]
             bank = psum.tile([P, GROUP], F32, name="bank")
-            for k in range(SLOTS_PER_BANK):
+            for k in range(2):
                 for g in range(TOKEN_PASSES):
                     nc.tensor.matmul_mx(
                         out=bank[:, COLS * k : COLS * (k + 1)],
-                        lhsT=s_codes[:, first + k, g, :].bitcast(FP4X4),
-                        lhsT_scale=s_plane[:, first + k, g, :],
+                        lhsT=s_codes[:, 2 * pair + k, g, :].bitcast(FP4X4),
+                        lhsT_scale=s_plane[:, 2 * pair + k, g, :],
                         rhs=u_codes[m, gi][:, g, 2 * COLS * chunk : 2 * COLS * (chunk + 1)].bitcast(FP4X4),
                         rhs_scale=u_plane[m, gi][:, g, COLS * chunk : COLS * (chunk + 1)],
                         start=(g == 0), stop=(g == TOKEN_PASSES - 1),
                     )
-            xs = slice(COLS // PACK * chunk, COLS // PACK * (chunk + 1))
-            ts = slice(first, first + SLOTS_PER_BANK)
-            sums = bank[:].rearrange("p (t x i) -> p i x t", t=SLOTS_PER_BANK, i=PACK)
-            dst = h_bf[gi, m, gj][:, :, xs, ts]
+            sums = bank[:].rearrange("p (t x) -> p x t", t=2)
+            dst = h_pairs[gi, m, gj, chunk][:, pair]
             if gi == gj:
-                nc.vector.tensor_tensor(out=dst, in0=sums, in1=shrink[:, :, xs, ts], op=ALU.mult)
+                sums = sums.rearrange("p (h s x) t -> p s h x t", s=2, x=8)
+                dst = dst.rearrange("p (h s x) t -> p s h x t", s=2, x=8)
+                nc.vector.tensor_tensor(out=dst[:, pair], in0=sums[:, pair], in1=shrink[:, 16 * chunk : 16 * (chunk + 1)], op=ALU.mult)
+                nc.scalar.activation(out=dst[:, 1 - pair], in_=sums[:, 1 - pair], func=ACT.Copy, scale=ALPHA)
             else:
                 nc.scalar.activation(out=dst, in_=sums, func=ACT.Copy, scale=ALPHA)
 
-        def result_bank(gi, half, t):
-            cols = slice(HALF_N * half, HALF_N * (half + 1))
+        def do_merge(gi, m, gj, chunk):
+            words = h_bf[gi, m, gj][:].bitcast(F32)[:, :, P // 2 * chunk : P // 2 * (chunk + 1), :]
+            pairs = h_pairs[gi, m, gj, chunk][:].bitcast(F32)
+            nc.vector.tensor_copy(
+                out=words.rearrange("p i (y l) u -> p y i l u", l=2),
+                in_=pairs.rearrange("p u (y l i) w -> p y i l (u w)", l=2, i=PACK),
+            )
+
+        def result_bank(gi, col0, width, t):
+            cols = slice(col0, col0 + width)
             if t == 0:
-                y_f32[gi, half] = new("y_f32%d%d" % (gi, half), [P, PACK, HALF_N], F32)
+                y_f32[gi, col0] = new("y_f32%d_%d" % (gi, col0), [P, PACK, width], F32)
             bank = psum.tile([P, GROUP], F32, name="bank")
-            terms = [(m, gj) for m in range(2) for gj in (1, 0)]
+            terms = [(0, 1), (0, 0), (1, 1), (1, 0)]
             for k, (m, gj) in enumerate(terms):
                 h_codes, h_plane = h_mx[gi, m, gj]
                 a_codes, a_plane = a_mx[m, gj]
                 nc.tensor.matmul_mx(
-                    out=bank[:, :HALF_N],
+                    out=bank[:, :width],
                     lhsT=h_codes[:, P * t : P * (t + 1)].bitcast(FP8X4), lhsT_scale=h_plane[:, P * t : P * (t + 1)],
                     rhs=a_codes[:, cols].bitcast(FP8X4), rhs_scale=a_plane[:, cols],
                     start=(k == 0), stop=(k == len(terms) - 1),
                 )
-            y = y_f32[gi, half]
+            y = y_f32[gi, col0]
             nc.vector.scalar_tensor_tensor(
-                out=y[:, t, :], in0=base_sb[gi][:, t, cols], scalar=lam_sb[:, gi, t : t + 1], in1=bank[:, :HALF_N],
+                out=y[:, t, :], in0=base_sb[gi][:, t, cols], scalar=lam_sb[:, gi, t : t + 1], in1=bank[:, :width],
                 op0=ALU.mult, op1=ALU.add,
             )
-            if t % 2 == 1:
+            if t == PACK - 1:
                 rows = out_0[GROUP * gi : GROUP * (gi + 1), cols].rearrange("(p t) n -> p t n", t=PACK)
-                nc.sync.dma_start(out=rows[:, t - 1 : t + 1, :], in_=y[:, t - 1 : t + 1, :])
+                nc.sync.dma_start(out=rows, in_=y[:])
 
-        def do_mix_y(gi, half, scalar_cols):
-            y_tile = new("y_bf%d%d" % (gi, half), [P, HALF_N, PACK], BF16)
-            y_bf[gi, half] = y_tile
-            y = y_f32[gi, half]
-            interleave(nc.scalar.copy, y_tile[:, :scalar_cols, :], y[:, :, :scalar_cols])
-            if scalar_cols < HALF_N:
+        def do_mix_y(gi, col0, scalar_cols):
+            y = y_f32[gi, col0]
+            width = y.shape[2]
+            y_tile = new("y_bf%d_%d" % (gi, col0), [P, width, PACK], BF16)
+            y_bf[gi, col0] = y_tile
+            if scalar_cols > 0:
+                interleave(nc.scalar.copy, y_tile[:, :scalar_cols, :], y[:, :, :scalar_cols])
+            if scalar_cols < width:
                 interleave(nc.vector.tensor_copy, y_tile[:, scalar_cols:, :], y[:, :, scalar_cols:])
 
-        def do_quant_y(gi, half):
-            cols = slice(HALF_N * half, HALF_N * (half + 1))
-            codes = new("y_codes%d%d" % (gi, half), [P, HALF_N], U32)
+        def do_quant_y(gi, col0):
+            width = y_bf[gi, col0].shape[1]
+            cols = slice(col0, col0 + width)
             nc.vector.quantize_mx(
-                out=codes[:].bitcast(FP8X4), scales=y_plane[gi][:, cols], in_=y_bf[gi, half][:].rearrange("p n t -> p (n t)")
+                out=y_codes[gi][:, cols].bitcast(FP8X4), scales=y_plane[gi][:, cols], in_=y_bf[gi, col0][:].rearrange("p n t -> p (n t)")
             )
             words = out_1[gi].rearrange("p n t -> p (n t)").bitcast(I32)
-            nc.sync.dma_start(out=words[:, cols], in_=codes[:].bitcast(I32))
-            if half == 1:
+            if (col0 + width) % HALF_N == 0:
+                half = slice(col0 + width - HALF_N, col0 + width)
+                nc.sync.dma_start(out=words[:, half], in_=y_codes[gi][:, half].bitcast(I32))
+            if col0 + width == N:
                 rows = out_2[gi].rearrange("(q r) n -> r q n", r=4)
                 for r in range(4):
-                    queue = nc.scalar if r % 2 else nc.sync
+                    queue = nc.scalar if gi == 1 and r < 3 else nc.sync
                     queue.dma_start(out=rows[r].bitcast(I32), in_=y_plane[gi][r:P:32, :].bitcast(I32))
 
         def gram(gi, m, gj, after):
@@ -238,30 +254,43 @@ def tile_regmean_merge_rhs_k5_kernel(
                 for job in after.get(unit, []):
                     job()
 
-        def result(gi, half, after):
+        def result(gi, col0, width, after):
             for t in range(PACK):
-                result_bank(gi, half, t)
+                result_bank(gi, col0, width, t)
                 for job in after.get(t, []):
                     job()
 
         s_copy, v_copy = nc.scalar.copy, nc.vector.tensor_copy
-        do_sort_v(0, 1)
         make_shrink()
-        gram(0, 0, 1, {0: [lambda: do_sort_v(0, 0)]})
-        gram(0, 0, 0, {0: [lambda: do_quant_h(0, 0, 1)], 1: [lambda: do_sort_v(1, 1)]})
+        do_sort_v(0, 1)
+        gram(0, 0, 1, {0: [lambda: do_sort_v(0, 0)], 1: [lambda: do_merge(0, 0, 1, 0)], 3: [lambda: do_merge(0, 0, 1, 1)]})
+        gram(0, 0, 0, {0: [lambda: do_quant_h(0, 0, 1)], 1: [lambda: do_sort_v(1, 1)], 2: [lambda: do_merge(0, 0, 0, 0)]})
         gram(0, 1, 1, {
-            0: [lambda: do_sort_v(1, 0), lambda: do_quant_h(0, 0, 0), lambda: do_mix_a(s_copy, 0, 1, 0)],
-            1: [lambda: do_mix_a(s_copy, 0, 1, 1)],
-            2: [lambda: do_mix_a(v_copy, 0, 0, 0), lambda: do_mix_a(v_copy, 0, 0, 1)],
-            3: [lambda: do_mix_a(s_copy, 1, 1, 0), lambda: do_mix_a(s_copy, 1, 1, 1),
-                lambda: do_mix_a(s_copy, 1, 0, 0), lambda: do_mix_a(s_copy, 1, 0, 1)],
+            0: [lambda: do_sort_v(1, 0), lambda: do_merge(0, 0, 0, 1), lambda: do_mix_a(v_copy, 0, 1, 0), lambda: do_quant_h(0, 0, 0)],
+            1: [lambda: do_merge(0, 1, 1, 0), lambda: do_mix_a(v_copy, 0, 1, 1)],
+            3: [lambda: do_merge(0, 1, 1, 1)],
         })
-        gram(0, 1, 0, {0: [lambda: do_quant_h(0, 1, 1)], 1: [lambda: do_quant_a(0, 1)], 2: [lambda: do_quant_a(0, 0)]})
-        gram(1, 0, 1, {0: [lambda: do_quant_h(0, 1, 0)], 2: [lambda: do_quant_a(1, 1)]})
-        gram(1, 0, 0, {0: [lambda: do_quant_a(1, 0), lambda: do_quant_h(1, 0, 1)]})
-        result(0, 0, {0: [lambda: do_quant_h(1, 0, 0)], 3: [lambda: do_mix_y(0, 0, HALF_N)]})
-        gram(1, 1, 1, {1: [lambda: do_quant_y(0, 0)]})
-        gram(1, 1, 0, {0: [lambda: do_quant_h(1, 1, 1)]})
-        result(0, 1, {0: [lambda: do_quant_h(1, 1, 0)], 3: [lambda: do_mix_y(0, 1, HALF_N)]})
-        result(1, 0, {1: [lambda: do_quant_y(0, 1)], 3: [lambda: do_mix_y(1, 0, HALF_N)]})
-        result(1, 1, {1: [lambda: do_quant_y(1, 0)], 3: [lambda: do_mix_y(1, 1, SCALAR_COLS), lambda: do_quant_y(1, 1)]})
+        gram(0, 1, 0, {
+            0: [lambda: do_quant_h(0, 1, 1), lambda: do_mix_a(s_copy, 0, 0, 0, 4)],
+            1: [lambda: do_quant_a(0, 1), lambda: do_mix_a(s_copy, 0, 0, 1, 4)],
+            2: [lambda: do_merge(0, 1, 0, 0), lambda: do_mix_a(s_copy, 0, 0, 2, 4)],
+            3: [lambda: do_mix_a(s_copy, 0, 0, 3, 4)],
+        })
+        gram(1, 0, 1, {
+            0: [lambda: do_merge(0, 1, 0, 1), lambda: do_mix_a(s_copy, 1, 1, 0, 4)],
+            1: [lambda: do_quant_h(0, 1, 0), lambda: do_mix_a(s_copy, 1, 1, 1, 4)],
+            2: [lambda: do_merge(1, 0, 1, 0), lambda: do_mix_a(s_copy, 1, 1, 2, 4)],
+            3: [lambda: do_quant_a(0, 0), lambda: do_mix_a(s_copy, 1, 1, 3, 4)],
+        })
+        gram(1, 0, 0, {
+            0: [lambda: do_mix_a(v_copy, 1, 0, 0), lambda: do_merge(1, 0, 1, 1), lambda: do_mix_a(v_copy, 1, 0, 1), lambda: do_quant_a(1, 1), lambda: do_quant_a(1, 0)],
+            1: [lambda: do_quant_h(1, 0, 1), lambda: do_merge(1, 0, 0, 0)],
+            3: [lambda: do_merge(1, 0, 0, 1)],
+        })
+        result(0, 0, 256, {0: [lambda: do_quant_h(1, 0, 0)], 3: [lambda: do_mix_y(0, 0, 256)]})
+        gram(1, 1, 1, {1: [lambda: do_quant_y(0, 0)], 2: [lambda: do_merge(1, 1, 1, 0)]})
+        gram(1, 1, 0, {0: [lambda: do_merge(1, 1, 1, 1)], 1: [lambda: do_quant_h(1, 1, 1), lambda: do_merge(1, 1, 0, 0)], 3: [lambda: do_merge(1, 1, 0, 1)]})
+        result(0, 256, 256, {0: [lambda: do_quant_h(1, 1, 0)], 3: [lambda: do_mix_y(0, 256, 256)]})
+        result(1, 0, 256, {3: [lambda: do_quant_y(0, 256), lambda: do_mix_y(1, 0, 128)]})
+        result(1, 256, 128, {3: [lambda: do_quant_y(1, 0), lambda: do_mix_y(1, 256, 128)]})
+        result(1, 384, 128, {3: [lambda: do_quant_y(1, 256), lambda: do_mix_y(1, 384, 0), lambda: do_quant_y(1, 384)]})

@@ -18,12 +18,15 @@ ACT = mybir.ActivationFunctionType
 ALU = mybir.AluOpType
 
 P = 128
-PACK = 4
-GROUP = P * PACK
-TOKEN_PASSES = T // GROUP
-HALF_N = N // 2
-COLS = 256
-SCALAR_COLS = 32
+SLOTS = 4
+HALF = P * SLOTS
+TOKEN_PASSES = T // HALF
+CHUNK = HALF // 2
+BANKS = 4
+WIDE, NARROW = N // 2, N // 4
+J_ORDER = (1, 0)
+H_BUFS = 3
+PAIR_BUFS = 4
 
 
 def tile_regmean_merge_rhs_k5_kernel(
@@ -31,179 +34,177 @@ def tile_regmean_merge_rhs_k5_kernel(
     a1, a2, base, lam, out_0, out_1, out_2,
 ):
     nc = tc.nc
-    u_words, v_words = (u1_words, u2_words), (v1_words, v2_words)
+    u_words, u_scales = (u1_words, u2_words), (u1_scales, u2_scales)
+    v_words, v_scales = (v1_words, v2_words), (v1_scales, v2_scales)
     weights = (a1, a2)
 
     with ExitStack() as ctx:
         keep = ctx.enter_context(tc.tile_pool(name="keep", bufs=1))
-        ring = ctx.enter_context(tc.tile_pool(name="ring", bufs=3))
+        ring = ctx.enter_context(tc.tile_pool(name="ring", bufs=H_BUFS))
         psum = ctx.enter_context(tc.psum_pool(name="psum", bufs=8))
         ctx.enter_context(tc.manual_schedule())
 
         def new(name, shape, dtype):
             return keep.tile(shape, dtype, name=name, align_bytes=64)
 
-        def load_codes(name, words, half):
-            codes = new(name, [P, TOKEN_PASSES, 2 * GROUP], U8)
-            src = words.rearrange("g p n -> p g n")[:, :, 2 * GROUP * half : 2 * GROUP * (half + 1)]
+        def load_codes(name, words, part, width):
+            codes = new(name, [P, TOKEN_PASSES, 2 * width], U8)
+            src = words.rearrange("g p n -> p g n")[:, :, 2 * width * part : 2 * width * (part + 1)]
             nc.sync.dma_start(out=codes[:].bitcast(I32), in_=src.bitcast(I32))
             return codes
 
-        def cleared_plane(name, width, engine=nc.vector):
-            plane = new(name, [P, TOKEN_PASSES, width], U8)
+        def cleared_plane(name, engine):
+            plane = new(name, [P, TOKEN_PASSES, HALF], U8)
             engine.memset(plane[:].bitcast(I32), 0)
             return plane
 
-        def load_scale_rows(queue, plane, scales, col0, rows):
-            width = plane.shape[2]
-            for r in rows:
-                src = scales.rearrange("g (q r) n -> r q g n", r=4)[r][:, :, col0 : col0 + width]
+        def load_scale_rows(queue, plane, scales, half):
+            rows = scales.rearrange("g (q r) n -> r q g n", r=4)
+            for r in range(4):
+                src = rows[r][:, :, HALF * half : HALF * (half + 1)]
                 queue.dma_start(out=plane[r:P:32, :, :].bitcast(I32), in_=src.bitcast(I32))
 
-        def sort_v(name, codes, plane):
-            s_codes = new(name + "_codes", [P, PACK, TOKEN_PASSES, 2 * P], U8)
-            s_plane = new(name + "_plane", [P, PACK, TOKEN_PASSES, P], U8)
-            nc.vector.tensor_copy(
-                out=s_codes[:].rearrange("p t g n -> p t (g n)").bitcast(I32).rearrange("p t (x a e) -> p x t a e", a=2, e=2),
-                in_=codes[:].rearrange("p g n -> p (g n)").bitcast(I32).rearrange("p (x a t e) -> p x t a e", a=2, t=4, e=2),
-            )
-            nc.vector.tensor_copy(
-                out=s_plane[:].bitcast(I32).rearrange("p t g (x w) -> p x g t w", w=4),
-                in_=plane.bitcast(I32).rearrange("p g (x w t) -> p x g t w", w=4, t=4),
-            )
-            return s_codes, s_plane
+        def load_v(m, gj):
+            v_plane[m, gj] = cleared_plane("v_plane%d%d" % (m, gj), nc.vector)
+            v_raw[m, gj] = load_codes("v_raw%d%d" % (m, gj), v_words[m], gj, HALF)
+            load_scale_rows(nc.sync, v_plane[m, gj], v_scales[m], gj)
 
-        def load_weight(m, g):
-            raw = new("a_raw%d%d" % (m, g), [P, PACK, N], BF16)
-            src = weights[m][GROUP * g : GROUP * (g + 1), :].rearrange("(x t b) n -> b x t n", t=4, b=4)
+        def load_u(m, gi):
+            u_plane[m, gi] = cleared_plane("u_plane%d%d" % (m, gi), nc.vector)
+            codes = load_codes("u_codes%d%d" % (m, gi), u_words[m], gi, HALF)
+            for chunk in range(2):
+                u_codes[m, gi, chunk] = codes[:, :, 2 * CHUNK * chunk : 2 * CHUNK * (chunk + 1)]
+            load_scale_rows(nc.sync, u_plane[m, gi], u_scales[m], gi)
+
+        def load_weight(m, gj):
+            raw = new("a_raw%d%d" % (m, gj), [P, SLOTS, N], BF16)
+            rows = weights[m][HALF * gj : HALF * (gj + 1), :].rearrange("(x t b) n -> b x t n", t=SLOTS, b=4)
             for b in range(4):
-                nc.sync.dma_start(out=raw[b:P:4, :, :], in_=src[b])
-            return raw
+                nc.sync.dma_start(out=raw[b:P:4, :, :], in_=rows[b])
+            a_raw[m, gj] = raw
+
+        v_plane = {(0, 1): cleared_plane("v_plane01", nc.gpsimd)}
+        u_plane = {(0, 0): cleared_plane("u_plane00", nc.vector)}
+        load_scale_rows(nc.scalar, v_plane[0, 1], v_scales[0], 1)
+        v_raw = {(0, 1): load_codes("v_raw01", v_words[0], 1, HALF)}
+        u_codes = {(0, 0, 0): load_codes("u_codes000", u_words[0], 0, CHUNK)[:]}
+        load_scale_rows(nc.sync, u_plane[0, 0], u_scales[0], 0)
+        u_codes[0, 0, 1] = load_codes("u_codes001", u_words[0], 1, CHUNK)[:]
+        ident = new("ident", [P, P], BF16)
+        make_identity(nc, ident[:])
+
+        a_raw = {}
+        load_v(0, 0)
+        load_v(1, 1)
+        load_u(1, 0)
+        load_v(1, 0)
+        load_u(0, 1)
+        for m in range(2):
+            for gj in J_ORDER:
+                load_weight(m, gj)
+        load_u(1, 1)
+        lam_sb = new("lam_sb", [P, 2, SLOTS], BF16)
+        nc.sync.dma_start(out=lam_sb[:], in_=lam.rearrange("(g p t) -> p g t", g=2, t=SLOTS))
+        base_sb = []
+        for gi in range(2):
+            base_half = new("base%d" % gi, [P, SLOTS, N], BF16)
+            rows = base[HALF * gi : HALF * (gi + 1), :].rearrange("(p t) n -> p t n", t=SLOTS)
+            nc.sync.dma_start(out=base_half[:], in_=rows)
+            base_sb.append(base_half)
+
+        shrink = new("shrink", [P, P // 4, 8, 2], BF16)
+        nc.vector.memset(shrink[:], ALPHA)
+        for l in range(2):
+            nc.scalar.activation(
+                out=shrink[:, :, 4 * l : 4 * (l + 1), l],
+                in_=ident[:].rearrange("p (h b) -> p h b", b=4),
+                func=ACT.Copy, scale=1.0 - ALPHA, bias=ALPHA,
+            )
+
+        v_sorted, a_words, a_mx, h_pairs, h_words, h_mx, y_f32, y_words = {}, {}, {}, {}, {}, {}, {}, {}
+        y_codes = [new("y_codes%d" % gi, [P, N], U32) for gi in range(2)]
+        y_plane = new("y_plane", [P, N], U8)
+
+        def sort_v(m, gj):
+            codes = new("v_codes%d%d" % (m, gj), [P, SLOTS, TOKEN_PASSES, 2 * P], U8)
+            plane = new("v_sorted_plane%d%d" % (m, gj), [P, SLOTS, TOKEN_PASSES, P], U8)
+            nc.vector.tensor_copy(
+                out=codes[:].rearrange("p t g n -> p t (g n)").bitcast(I32).rearrange("p t (y a e) -> p y t a e", a=2, e=2),
+                in_=v_raw[m, gj][:].rearrange("p g n -> p (g n)").bitcast(I32).rearrange("p (y a t e) -> p y t a e", a=2, t=SLOTS, e=2),
+            )
+            nc.vector.tensor_copy(
+                out=plane[:].bitcast(I32).rearrange("p t g (y w) -> p y g t w", w=4),
+                in_=v_plane[m, gj][:].bitcast(I32).rearrange("p g (y w t) -> p y g t w", w=4, t=SLOTS),
+            )
+            v_sorted[m, gj] = codes, plane
 
         def interleave(copy, dst, src):
-            copy(
-                out=dst.rearrange("p (c i) t -> p c t i", i=4),
-                in_=src.rearrange("p t (c i) -> p c t i", i=4),
-            )
+            copy(out=dst.rearrange("p (c e) t -> p c t e", e=4), in_=src.rearrange("p t (c e) -> p c t e", e=4))
 
-        def quantise(name, src, width):
+        def quantise(name, src):
+            width = src.shape[1] // SLOTS
             codes = new(name + "_codes", [P, width], U32)
             plane = new(name + "_plane", [P, width], U8)
             nc.vector.quantize_mx(out=codes[:].bitcast(FP8X4), scales=plane[:], in_=src)
             return codes, plane
 
-        v1_plane = {1: cleared_plane("v1_plane1", GROUP, nc.gpsimd)}
-        u1_plane = {0: cleared_plane("u1_plane0", GROUP)}
-        load_scale_rows(nc.scalar, v1_plane[1], v1_scales, GROUP, range(4))
-        v_raw = {(0, 1): load_codes("v_raw01", v_words[0], 1)}
-        u_codes = {(0, 0): load_codes("u_codes00", u_words[0], 0)}
-        load_scale_rows(nc.sync, u1_plane[0], u1_scales, 0, range(4))
-        ident = new("ident", [P, P], BF16)
-        make_identity(nc, ident[:])
+        def interleave_a(copy, m, gj, part, parts):
+            if part == 0:
+                a_words[m, gj] = new("a_words%d%d" % (m, gj), [P, N, SLOTS], BF16)
+            cols = slice(N // parts * part, N // parts * (part + 1))
+            interleave(copy, a_words[m, gj][:, cols, :], a_raw[m, gj][:, :, cols])
 
-        v1_plane[0] = cleared_plane("v1_plane0", GROUP)
-        v2_plane = cleared_plane("v2_plane", D)
-        u2_plane = cleared_plane("u2_plane", D)
-        u1_plane[1] = cleared_plane("u1_plane1", GROUP)
-        shrink = new("shrink", [P, 32, 8, 2], BF16)
+        def quantise_a(m, gj):
+            a_mx[m, gj] = quantise("a%d%d" % (m, gj), a_words[m, gj][:].rearrange("p n t -> p (n t)"))
 
-        def make_shrink():
-            nc.vector.memset(shrink[:], ALPHA)
-            for l in range(2):
-                nc.scalar.activation(
-                    out=shrink[:, :, PACK * l : PACK * (l + 1), l],
-                    in_=ident[:].rearrange("p (h i) -> p h i", i=PACK),
-                    func=ACT.Copy, scale=1.0 - ALPHA, bias=ALPHA,
-                )
-
-        v_raw[0, 0] = load_codes("v_raw00", v_words[0], 0)
-        load_scale_rows(nc.sync, v1_plane[0], v1_scales, 0, range(4))
-        load_scale_rows(nc.sync, v2_plane, v2_scales, 0, range(4))
-        load_scale_rows(nc.sync, u2_plane, u2_scales, 0, range(4))
-        v_raw[1, 1] = load_codes("v_raw11", v_words[1], 1)
-        u_codes[1, 0] = load_codes("u_codes10", u_words[1], 0)
-        v_raw[1, 0] = load_codes("v_raw10", v_words[1], 0)
-        a_raw = {(m, g): load_weight(m, g) for m in range(2) for g in (1, 0)}
-        u_codes[0, 1] = load_codes("u_codes01", u_words[0], 1)
-        load_scale_rows(nc.sync, u1_plane[1], u1_scales, GROUP, range(4))
-        lam_sb = new("lam_sb", [P, 2, PACK], BF16)
-        nc.sync.dma_start(out=lam_sb[:], in_=lam.rearrange("(g p t) -> p g t", g=2, t=PACK))
-        base_sb = []
-        for g in range(2):
-            base_g = new("base%d" % g, [P, PACK, N], BF16)
-            nc.sync.dma_start(out=base_g[:], in_=base[GROUP * g : GROUP * (g + 1), :].rearrange("(p t) n -> p t n", t=PACK))
-            base_sb.append(base_g)
-        u_codes[1, 1] = load_codes("u_codes11", u_words[1], 1)
-
-        def half_of(plane, half):
-            return plane[:, :, GROUP * half : GROUP * (half + 1)]
-
-        u_plane = {(0, 0): u1_plane[0][:], (0, 1): u1_plane[1][:], (1, 0): half_of(u2_plane, 0), (1, 1): half_of(u2_plane, 1)}
-        v_plane = {(0, 0): v1_plane[0][:], (0, 1): v1_plane[1][:], (1, 0): half_of(v2_plane, 0), (1, 1): half_of(v2_plane, 1)}
-
-        v_sorted, a_mixed, a_mx, h_bf, h_mx, y_f32, y_bf, h_pairs = {}, {}, {}, {}, {}, {}, {}, {}
-        y_codes = [new("y_codes%d" % g, [P, N], U32) for g in range(2)]
-        y_plane = [new("y_plane%d" % g, [P, N], U8) for g in range(2)]
-
-        def do_sort_v(m, gj):
-            v_sorted[m, gj] = sort_v("v%d%d" % (m, gj), v_raw[m, gj], v_plane[m, gj])
-
-        def do_mix_a(copy, m, g, half, parts=2):
-            if half == 0:
-                a_mixed[m, g] = new("a_mixed%d%d" % (m, g), [P, N, PACK], BF16)
-            cols = slice(N // parts * half, N // parts * (half + 1))
-            interleave(copy, a_mixed[m, g][:, cols, :], a_raw[m, g][:, :, cols])
-
-        def do_quant_a(m, g):
-            a_mx[m, g] = quantise("a%d%d" % (m, g), a_mixed[m, g][:].rearrange("p n t -> p (n t)"), N)
-
-        def do_quant_h(gi, m, gj):
-            h_mx[gi, m, gj] = quantise("h%d%d%d" % (gi, m, gj), h_bf[gi, m, gj][:].rearrange("p i x t -> p (i x t)"), GROUP)
-
-        def gram_bank(gi, m, gj, unit):
+        def gram_bank(quadrant, unit):
+            gi, m, gj = quadrant
             chunk, pair = divmod(unit, 2)
             if unit == 0:
-                h_tile = ring.tile([P, PACK, P, PACK], BF16, name="h_tile", align_bytes=64)
-                h_bf[gi, m, gj] = h_tile
+                h_words[quadrant] = ring.tile([P, SLOTS, P, SLOTS], BF16, name="h_words", align_bytes=64)
             if pair == 0:
-                h_stage = ring.tile([P, 2, COLS, 2], BF16, name="h_stage", align_bytes=64, bufs=4)
-                h_pairs[gi, m, gj, chunk] = h_stage
-            s_codes, s_plane = v_sorted[m, gj]
-            bank = psum.tile([P, GROUP], F32, name="bank")
+                h_pairs[quadrant, chunk] = ring.tile([P, 2, CHUNK, 2], BF16, name="h_pairs", align_bytes=64, bufs=PAIR_BUFS)
+            v_codes, v_sorted_plane = v_sorted[m, gj]
+            bank = psum.tile([P, HALF], F32, name="bank")
             for k in range(2):
                 for g in range(TOKEN_PASSES):
                     nc.tensor.matmul_mx(
-                        out=bank[:, COLS * k : COLS * (k + 1)],
-                        lhsT=s_codes[:, 2 * pair + k, g, :].bitcast(FP4X4),
-                        lhsT_scale=s_plane[:, 2 * pair + k, g, :],
-                        rhs=u_codes[m, gi][:, g, 2 * COLS * chunk : 2 * COLS * (chunk + 1)].bitcast(FP4X4),
-                        rhs_scale=u_plane[m, gi][:, g, COLS * chunk : COLS * (chunk + 1)],
+                        out=bank[:, CHUNK * k : CHUNK * (k + 1)],
+                        lhsT=v_codes[:, 2 * pair + k, g, :].bitcast(FP4X4),
+                        lhsT_scale=v_sorted_plane[:, 2 * pair + k, g, :],
+                        rhs=u_codes[m, gi, chunk][:, g, :].bitcast(FP4X4),
+                        rhs_scale=u_plane[m, gi][:, g, CHUNK * chunk : CHUNK * (chunk + 1)],
                         start=(g == 0), stop=(g == TOKEN_PASSES - 1),
                     )
-            sums = bank[:].rearrange("p (t x) -> p x t", t=2)
-            dst = h_pairs[gi, m, gj, chunk][:, pair]
+            sums = bank[:].rearrange("p (k x) -> p x k", k=2)
+            dst = h_pairs[quadrant, chunk][:, pair]
             if gi == gj:
-                sums = sums.rearrange("p (h s x) t -> p s h x t", s=2, x=8)
-                dst = dst.rearrange("p (h s x) t -> p s h x t", s=2, x=8)
-                nc.vector.tensor_tensor(out=dst[:, pair], in0=sums[:, pair], in1=shrink[:, 16 * chunk : 16 * (chunk + 1)], op=ALU.mult)
+                sums = sums.rearrange("p (h s c) k -> p s h c k", s=2, c=8)
+                dst = dst.rearrange("p (h s c) k -> p s h c k", s=2, c=8)
+                factors = shrink[:, CHUNK // 16 * chunk : CHUNK // 16 * (chunk + 1)]
+                nc.vector.tensor_tensor(out=dst[:, pair], in0=sums[:, pair], in1=factors, op=ALU.mult)
                 nc.scalar.activation(out=dst[:, 1 - pair], in_=sums[:, 1 - pair], func=ACT.Copy, scale=ALPHA)
             else:
                 nc.scalar.activation(out=dst, in_=sums, func=ACT.Copy, scale=ALPHA)
 
-        def do_merge(gi, m, gj, chunk):
-            words = h_bf[gi, m, gj][:].bitcast(F32)[:, :, P // 2 * chunk : P // 2 * (chunk + 1), :]
-            pairs = h_pairs[gi, m, gj, chunk][:].bitcast(F32)
+        def join_pairs(quadrant, chunk):
+            words = h_words[quadrant][:].bitcast(F32)[:, :, P // 2 * chunk : P // 2 * (chunk + 1), :]
+            pairs = h_pairs[quadrant, chunk][:].bitcast(F32)
             nc.vector.tensor_copy(
-                out=words.rearrange("p i (y l) u -> p y i l u", l=2),
-                in_=pairs.rearrange("p u (y l i) w -> p y i l (u w)", l=2, i=PACK),
+                out=words.rearrange("p b (y l) u -> p y b l u", l=2),
+                in_=pairs.rearrange("p u (y l b) w -> p y b l (u w)", l=2, b=4),
             )
 
-        def result_bank(gi, col0, width, t):
+        def quantise_h(quadrant):
+            h_mx[quadrant] = quantise("h%d%d%d" % quadrant, h_words[quadrant][:].rearrange("p b x t -> p (b x t)"))
+
+        def result_bank(job, t):
+            gi, col0, width = job
             cols = slice(col0, col0 + width)
             if t == 0:
-                y_f32[gi, col0] = new("y_f32%d_%d" % (gi, col0), [P, PACK, width], F32)
-            bank = psum.tile([P, GROUP], F32, name="bank")
-            terms = [(0, 1), (0, 0), (1, 1), (1, 0)]
+                y_f32[job] = new("y_f32_%d_%d" % (gi, col0), [P, SLOTS, width], F32)
+            bank = psum.tile([P, HALF], F32, name="bank")
+            terms = [(m, gj) for m in range(2) for gj in J_ORDER]
             for k, (m, gj) in enumerate(terms):
                 h_codes, h_plane = h_mx[gi, m, gj]
                 a_codes, a_plane = a_mx[m, gj]
@@ -213,84 +214,115 @@ def tile_regmean_merge_rhs_k5_kernel(
                     rhs=a_codes[:, cols].bitcast(FP8X4), rhs_scale=a_plane[:, cols],
                     start=(k == 0), stop=(k == len(terms) - 1),
                 )
-            y = y_f32[gi, col0]
+            y = y_f32[job]
             nc.vector.scalar_tensor_tensor(
                 out=y[:, t, :], in0=base_sb[gi][:, t, cols], scalar=lam_sb[:, gi, t : t + 1], in1=bank[:, :width],
                 op0=ALU.mult, op1=ALU.add,
             )
-            if t == PACK - 1:
-                rows = out_0[GROUP * gi : GROUP * (gi + 1), cols].rearrange("(p t) n -> p t n", t=PACK)
-                nc.sync.dma_start(out=rows, in_=y[:])
+            slots_per_store = N // width
+            if (t + 1) % slots_per_store == 0:
+                ts = slice(t + 1 - slots_per_store, t + 1)
+                rows = out_0[HALF * gi : HALF * (gi + 1), cols].rearrange("(p t) n -> p t n", t=SLOTS)
+                nc.sync.dma_start(out=rows[:, ts, :], in_=y[:, ts, :])
 
-        def do_mix_y(gi, col0, scalar_cols):
-            y = y_f32[gi, col0]
-            width = y.shape[2]
-            y_tile = new("y_bf%d_%d" % (gi, col0), [P, width, PACK], BF16)
-            y_bf[gi, col0] = y_tile
+        def interleave_y(job, scalar_cols):
+            gi, col0, width = job
+            y = y_f32[job]
+            y_words[job] = new("y_words_%d_%d" % (gi, col0), [P, width, SLOTS], BF16)
             if scalar_cols > 0:
-                interleave(nc.scalar.copy, y_tile[:, :scalar_cols, :], y[:, :, :scalar_cols])
+                interleave(nc.scalar.copy, y_words[job][:, :scalar_cols, :], y[:, :, :scalar_cols])
             if scalar_cols < width:
-                interleave(nc.vector.tensor_copy, y_tile[:, scalar_cols:, :], y[:, :, scalar_cols:])
+                interleave(nc.vector.tensor_copy, y_words[job][:, scalar_cols:, :], y[:, :, scalar_cols:])
 
-        def do_quant_y(gi, col0):
-            width = y_bf[gi, col0].shape[1]
+        def quantise_y(job):
+            gi, col0, width = job
             cols = slice(col0, col0 + width)
             nc.vector.quantize_mx(
-                out=y_codes[gi][:, cols].bitcast(FP8X4), scales=y_plane[gi][:, cols], in_=y_bf[gi, col0][:].rearrange("p n t -> p (n t)")
+                out=y_codes[gi][:, cols].bitcast(FP8X4), scales=y_plane[4 * gi :, cols],
+                in_=y_words[job][:].rearrange("p n t -> p (n t)"),
             )
-            words = out_1[gi].rearrange("p n t -> p (n t)").bitcast(I32)
-            if (col0 + width) % HALF_N == 0:
-                half = slice(col0 + width - HALF_N, col0 + width)
-                nc.sync.dma_start(out=words[:, half], in_=y_codes[gi][:, half].bitcast(I32))
-            if col0 + width == N:
-                rows = out_2[gi].rearrange("(q r) n -> r q n", r=4)
-                for r in range(4):
-                    queue = nc.scalar if gi == 1 and r < 3 else nc.sync
-                    queue.dma_start(out=rows[r].bitcast(I32), in_=y_plane[gi][r:P:32, :].bitcast(I32))
+            if (col0 + width) % WIDE == 0:
+                done = slice(col0 + width - WIDE, col0 + width)
+                words = out_1[gi].rearrange("p n t -> p (n t)").bitcast(I32)
+                nc.sync.dma_start(out=words[:, done], in_=y_codes[gi][:, done].bitcast(I32))
 
-        def gram(gi, m, gj, after):
-            for unit in range(4):
-                gram_bank(gi, m, gj, unit)
-                for job in after.get(unit, []):
-                    job()
+        def store_y_plane():
+            rows = out_2.rearrange("g (q r) n -> q g r n", r=4).bitcast(I32)
+            for q in range(4):
+                queue = nc.sync if q == 3 else nc.scalar
+                queue.dma_start(out=rows[q], in_=y_plane[32 * q : 32 * q + 8, :].bitcast(I32))
 
-        def result(gi, col0, width, after):
-            for t in range(PACK):
-                result_bank(gi, col0, width, t)
-                for job in after.get(t, []):
-                    job()
-
+        quadrants = [(gi, m, gj) for gi in range(2) for m in range(2) for gj in J_ORDER]
         s_copy, v_copy = nc.scalar.copy, nc.vector.tensor_copy
-        make_shrink()
-        do_sort_v(0, 1)
-        gram(0, 0, 1, {0: [lambda: do_sort_v(0, 0)], 1: [lambda: do_merge(0, 0, 1, 0)], 3: [lambda: do_merge(0, 0, 1, 1)]})
-        gram(0, 0, 0, {0: [lambda: do_quant_h(0, 0, 1)], 1: [lambda: do_sort_v(1, 1)], 2: [lambda: do_merge(0, 0, 0, 0)]})
-        gram(0, 1, 1, {
-            0: [lambda: do_sort_v(1, 0), lambda: do_merge(0, 0, 0, 1), lambda: do_mix_a(v_copy, 0, 1, 0), lambda: do_quant_h(0, 0, 0)],
-            1: [lambda: do_merge(0, 1, 1, 0), lambda: do_mix_a(v_copy, 0, 1, 1)],
-            3: [lambda: do_merge(0, 1, 1, 1)],
-        })
-        gram(0, 1, 0, {
-            0: [lambda: do_quant_h(0, 1, 1), lambda: do_mix_a(s_copy, 0, 0, 0, 4)],
-            1: [lambda: do_quant_a(0, 1), lambda: do_mix_a(s_copy, 0, 0, 1, 4)],
-            2: [lambda: do_merge(0, 1, 0, 0), lambda: do_mix_a(s_copy, 0, 0, 2, 4)],
-            3: [lambda: do_mix_a(s_copy, 0, 0, 3, 4)],
-        })
-        gram(1, 0, 1, {
-            0: [lambda: do_merge(0, 1, 0, 1), lambda: do_mix_a(s_copy, 1, 1, 0, 4)],
-            1: [lambda: do_quant_h(0, 1, 0), lambda: do_mix_a(s_copy, 1, 1, 1, 4)],
-            2: [lambda: do_merge(1, 0, 1, 0), lambda: do_mix_a(s_copy, 1, 1, 2, 4)],
-            3: [lambda: do_quant_a(0, 0), lambda: do_mix_a(s_copy, 1, 1, 3, 4)],
-        })
-        gram(1, 0, 0, {
-            0: [lambda: do_mix_a(v_copy, 1, 0, 0), lambda: do_merge(1, 0, 1, 1), lambda: do_mix_a(v_copy, 1, 0, 1), lambda: do_quant_a(1, 1), lambda: do_quant_a(1, 0)],
-            1: [lambda: do_quant_h(1, 0, 1), lambda: do_merge(1, 0, 0, 0)],
-            3: [lambda: do_merge(1, 0, 0, 1)],
-        })
-        result(0, 0, 256, {0: [lambda: do_quant_h(1, 0, 0)], 3: [lambda: do_mix_y(0, 0, 256)]})
-        gram(1, 1, 1, {1: [lambda: do_quant_y(0, 0)], 2: [lambda: do_merge(1, 1, 1, 0)]})
-        gram(1, 1, 0, {0: [lambda: do_merge(1, 1, 1, 1)], 1: [lambda: do_quant_h(1, 1, 1), lambda: do_merge(1, 1, 0, 0)], 3: [lambda: do_merge(1, 1, 0, 1)]})
-        result(0, 256, 256, {0: [lambda: do_quant_h(1, 1, 0)], 3: [lambda: do_mix_y(0, 256, 256)]})
-        result(1, 0, 256, {3: [lambda: do_quant_y(0, 256), lambda: do_mix_y(1, 0, 128)]})
-        result(1, 256, 128, {3: [lambda: do_quant_y(1, 0), lambda: do_mix_y(1, 256, 128)]})
-        result(1, 384, 128, {3: [lambda: do_quant_y(1, 256), lambda: do_mix_y(1, 384, 0), lambda: do_quant_y(1, 384)]})
+
+        def finish_quadrant(quadrant, unit):
+            if unit == 0:
+                join_pairs(quadrant, 1)
+            if unit == 1:
+                quantise_h(quadrant)
+
+        def gram_step(index, beside, follows_quadrant=True):
+            for unit in range(BANKS):
+                gram_bank(quadrants[index], unit)
+                if follows_quadrant:
+                    finish_quadrant(quadrants[index - 1], unit)
+                if unit == 2:
+                    join_pairs(quadrants[index], 0)
+                beside(unit)
+
+        def result_step(job, quadrant_before=None):
+            for t in range(BANKS):
+                result_bank(job, t)
+                if quadrant_before is not None:
+                    finish_quadrant(quadrant_before, t)
+
+        def sort_next_v(index):
+            following = quadrants[index + 1]
+            return lambda unit: sort_v(following[1], following[2]) if unit == 0 else None
+
+        def beside_quadrant_3(unit):
+            interleave_a(s_copy, 0, 1, unit, BANKS)
+            if unit >= 2:
+                interleave_a(v_copy, 0, 0, unit - 2, 2)
+
+        def beside_quadrant_4(unit):
+            interleave_a(s_copy, 1, 1, unit, BANKS)
+            if unit >= 2:
+                quantise_a(0, J_ORDER[unit - 2])
+
+        def beside_quadrant_5(unit):
+            if unit < 2:
+                interleave_a(v_copy, 1, 0, unit, 2)
+            if unit == 2:
+                quantise_a(1, 1)
+
+        def beside_quadrant_6(unit):
+            if unit == 0:
+                quantise_a(1, 0)
+
+        jobs = [(0, 0, WIDE), (0, WIDE, WIDE), (1, 0, WIDE), (1, WIDE, NARROW), (1, WIDE + NARROW, NARROW)]
+
+        def planes_of_first_job(unit):
+            if unit == 0:
+                interleave_y(jobs[0], 0)
+            if unit == 1:
+                quantise_y(jobs[0])
+
+        sort_v(0, 1)
+        gram_step(0, sort_next_v(0), follows_quadrant=False)
+        gram_step(1, sort_next_v(1))
+        gram_step(2, sort_next_v(2))
+        gram_step(3, beside_quadrant_3)
+        gram_step(4, beside_quadrant_4)
+        gram_step(5, beside_quadrant_5)
+        gram_step(6, beside_quadrant_6)
+        result_step(jobs[0], quadrants[6])
+        gram_step(7, planes_of_first_job, follows_quadrant=False)
+        result_step(jobs[1], quadrants[7])
+        interleave_y(jobs[1], WIDE)
+        for k, scalar_cols in ((2, NARROW), (3, NARROW), (4, 0)):
+            result_step(jobs[k])
+            quantise_y(jobs[k - 1])
+            interleave_y(jobs[k], scalar_cols)
+        quantise_y(jobs[4])
+        store_y_plane()

from contextlib import ExitStack

import concourse.mybir as mybir
from concourse.masks import make_identity

D, T, N = 1024, 1536, 512
ALPHA = 0.75
FLOPS = 2 * (2 * D * D * T + 2 * D * D * N)

F32 = mybir.dt.float32
BF16 = mybir.dt.bfloat16
I32 = mybir.dt.int32
U32 = mybir.dt.uint32
U8 = mybir.dt.uint8
FP8X4 = mybir.dt.float8_e4m3fn_x4
FP4X4 = mybir.dt.float4_e2m1fn_x4
ACT = mybir.ActivationFunctionType
ALU = mybir.AluOpType

P = 128
SLOTS = 4
HALF = P * SLOTS
TOKEN_PASSES = T // HALF
CHUNK = HALF // 2
BANKS = 4
WIDE, NARROW = N // 2, N // 4
J_ORDER = (1, 0)
H_BUFS = 3
PAIR_BUFS = 4


def tile_regmean_merge_rhs_k5_kernel(
    tc, u1_words, u1_scales, v1_words, v1_scales, u2_words, u2_scales, v2_words, v2_scales,
    a1, a2, base, lam, out_0, out_1, out_2,
):
    nc = tc.nc
    u_words, u_scales = (u1_words, u2_words), (u1_scales, u2_scales)
    v_words, v_scales = (v1_words, v2_words), (v1_scales, v2_scales)
    weights = (a1, a2)

    with ExitStack() as ctx:
        keep = ctx.enter_context(tc.tile_pool(name="keep", bufs=1))
        ring = ctx.enter_context(tc.tile_pool(name="ring", bufs=H_BUFS))
        psum = ctx.enter_context(tc.psum_pool(name="psum", bufs=8))
        ctx.enter_context(tc.manual_schedule())

        def new(name, shape, dtype):
            return keep.tile(shape, dtype, name=name, align_bytes=64)

        def load_codes(name, words, part, width):
            codes = new(name, [P, TOKEN_PASSES, 2 * width], U8)
            src = words.rearrange("g p n -> p g n")[:, :, 2 * width * part : 2 * width * (part + 1)]
            nc.sync.dma_start(out=codes[:].bitcast(I32), in_=src.bitcast(I32))
            return codes

        def cleared_plane(name, engine):
            plane = new(name, [P, TOKEN_PASSES, HALF], U8)
            engine.memset(plane[:].bitcast(I32), 0)
            return plane

        def load_scale_rows(queue, plane, scales, half):
            rows = scales.rearrange("g (q r) n -> r q g n", r=4)
            for r in range(4):
                src = rows[r][:, :, HALF * half : HALF * (half + 1)]
                queue.dma_start(out=plane[r:P:32, :, :].bitcast(I32), in_=src.bitcast(I32))

        def load_v(m, gj):
            v_plane[m, gj] = cleared_plane("v_plane%d%d" % (m, gj), nc.vector)
            v_raw[m, gj] = load_codes("v_raw%d%d" % (m, gj), v_words[m], gj, HALF)
            load_scale_rows(nc.sync, v_plane[m, gj], v_scales[m], gj)

        def load_u(m, gi):
            u_plane[m, gi] = cleared_plane("u_plane%d%d" % (m, gi), nc.vector)
            codes = load_codes("u_codes%d%d" % (m, gi), u_words[m], gi, HALF)
            for chunk in range(2):
                u_codes[m, gi, chunk] = codes[:, :, 2 * CHUNK * chunk : 2 * CHUNK * (chunk + 1)]
            load_scale_rows(nc.sync, u_plane[m, gi], u_scales[m], gi)

        def load_weight(m, gj):
            raw = new("a_raw%d%d" % (m, gj), [P, SLOTS, N], BF16)
            rows = weights[m][HALF * gj : HALF * (gj + 1), :].rearrange("(x t b) n -> b x t n", t=SLOTS, b=4)
            for b in range(4):
                nc.sync.dma_start(out=raw[b:P:4, :, :], in_=rows[b])
            a_raw[m, gj] = raw

        v_plane = {(0, 1): cleared_plane("v_plane01", nc.gpsimd)}
        u_plane = {(0, 0): cleared_plane("u_plane00", nc.vector)}
        load_scale_rows(nc.scalar, v_plane[0, 1], v_scales[0], 1)
        v_raw = {(0, 1): load_codes("v_raw01", v_words[0], 1, HALF)}
        u_codes = {(0, 0, 0): load_codes("u_codes000", u_words[0], 0, CHUNK)[:]}
        load_scale_rows(nc.sync, u_plane[0, 0], u_scales[0], 0)
        u_codes[0, 0, 1] = load_codes("u_codes001", u_words[0], 1, CHUNK)[:]
        ident = new("ident", [P, P], BF16)
        make_identity(nc, ident[:])

        a_raw = {}
        load_v(0, 0)
        load_v(1, 1)
        load_u(1, 0)
        load_v(1, 0)
        load_u(0, 1)
        for m in range(2):
            for gj in J_ORDER:
                load_weight(m, gj)
        load_u(1, 1)
        lam_sb = new("lam_sb", [P, 2, SLOTS], BF16)
        nc.sync.dma_start(out=lam_sb[:], in_=lam.rearrange("(g p t) -> p g t", g=2, t=SLOTS))
        base_sb = []
        for gi in range(2):
            base_half = new("base%d" % gi, [P, SLOTS, N], BF16)
            rows = base[HALF * gi : HALF * (gi + 1), :].rearrange("(p t) n -> p t n", t=SLOTS)
            nc.sync.dma_start(out=base_half[:], in_=rows)
            base_sb.append(base_half)

        shrink = new("shrink", [P, P // 4, 8, 2], BF16)
        nc.vector.memset(shrink[:], ALPHA)
        for l in range(2):
            nc.scalar.activation(
                out=shrink[:, :, 4 * l : 4 * (l + 1), l],
                in_=ident[:].rearrange("p (h b) -> p h b", b=4),
                func=ACT.Copy, scale=1.0 - ALPHA, bias=ALPHA,
            )

        v_sorted, a_words, a_mx, h_pairs, h_words, h_mx, y_f32, y_words = {}, {}, {}, {}, {}, {}, {}, {}
        y_codes = [new("y_codes%d" % gi, [P, N], U32) for gi in range(2)]
        y_plane = new("y_plane", [P, N], U8)

        def sort_v(m, gj):
            codes = new("v_codes%d%d" % (m, gj), [P, SLOTS, TOKEN_PASSES, 2 * P], U8)
            plane = new("v_sorted_plane%d%d" % (m, gj), [P, SLOTS, TOKEN_PASSES, P], U8)
            nc.vector.tensor_copy(
                out=codes[:].rearrange("p t g n -> p t (g n)").bitcast(I32).rearrange("p t (y a e) -> p y t a e", a=2, e=2),
                in_=v_raw[m, gj][:].rearrange("p g n -> p (g n)").bitcast(I32).rearrange("p (y a t e) -> p y t a e", a=2, t=SLOTS, e=2),
            )
            nc.vector.tensor_copy(
                out=plane[:].bitcast(I32).rearrange("p t g (y w) -> p y g t w", w=4),
                in_=v_plane[m, gj][:].bitcast(I32).rearrange("p g (y w t) -> p y g t w", w=4, t=SLOTS),
            )
            v_sorted[m, gj] = codes, plane

        def interleave(copy, dst, src):
            copy(out=dst.rearrange("p (c e) t -> p c t e", e=4), in_=src.rearrange("p t (c e) -> p c t e", e=4))

        def quantise(name, src):
            width = src.shape[1] // SLOTS
            codes = new(name + "_codes", [P, width], U32)
            plane = new(name + "_plane", [P, width], U8)
            nc.vector.quantize_mx(out=codes[:].bitcast(FP8X4), scales=plane[:], in_=src)
            return codes, plane

        def interleave_a(copy, m, gj, part, parts):
            if part == 0:
                a_words[m, gj] = new("a_words%d%d" % (m, gj), [P, N, SLOTS], BF16)
            cols = slice(N // parts * part, N // parts * (part + 1))
            interleave(copy, a_words[m, gj][:, cols, :], a_raw[m, gj][:, :, cols])

        def quantise_a(m, gj):
            a_mx[m, gj] = quantise("a%d%d" % (m, gj), a_words[m, gj][:].rearrange("p n t -> p (n t)"))

        def gram_bank(quadrant, unit):
            gi, m, gj = quadrant
            chunk, pair = divmod(unit, 2)
            if unit == 0:
                h_words[quadrant] = ring.tile([P, SLOTS, P, SLOTS], BF16, name="h_words", align_bytes=64)
            if pair == 0:
                h_pairs[quadrant, chunk] = ring.tile([P, 2, CHUNK, 2], BF16, name="h_pairs", align_bytes=64, bufs=PAIR_BUFS)
            v_codes, v_sorted_plane = v_sorted[m, gj]
            bank = psum.tile([P, HALF], F32, name="bank")
            for k in range(2):
                for g in range(TOKEN_PASSES):
                    nc.tensor.matmul_mx(
                        out=bank[:, CHUNK * k : CHUNK * (k + 1)],
                        lhsT=v_codes[:, 2 * pair + k, g, :].bitcast(FP4X4),
                        lhsT_scale=v_sorted_plane[:, 2 * pair + k, g, :],
                        rhs=u_codes[m, gi, chunk][:, g, :].bitcast(FP4X4),
                        rhs_scale=u_plane[m, gi][:, g, CHUNK * chunk : CHUNK * (chunk + 1)],
                        start=(g == 0), stop=(g == TOKEN_PASSES - 1),
                    )
            sums = bank[:].rearrange("p (k x) -> p x k", k=2)
            dst = h_pairs[quadrant, chunk][:, pair]
            if gi == gj:
                sums = sums.rearrange("p (h s c) k -> p s h c k", s=2, c=8)
                dst = dst.rearrange("p (h s c) k -> p s h c k", s=2, c=8)
                factors = shrink[:, CHUNK // 16 * chunk : CHUNK // 16 * (chunk + 1)]
                nc.vector.tensor_tensor(out=dst[:, pair], in0=sums[:, pair], in1=factors, op=ALU.mult)
                nc.scalar.activation(out=dst[:, 1 - pair], in_=sums[:, 1 - pair], func=ACT.Copy, scale=ALPHA)
            else:
                nc.scalar.activation(out=dst, in_=sums, func=ACT.Copy, scale=ALPHA)

        def join_pairs(quadrant, chunk):
            words = h_words[quadrant][:].bitcast(F32)[:, :, P // 2 * chunk : P // 2 * (chunk + 1), :]
            pairs = h_pairs[quadrant, chunk][:].bitcast(F32)
            nc.vector.tensor_copy(
                out=words.rearrange("p b (y l) u -> p y b l u", l=2),
                in_=pairs.rearrange("p u (y l b) w -> p y b l (u w)", l=2, b=4),
            )

        def quantise_h(quadrant):
            h_mx[quadrant] = quantise("h%d%d%d" % quadrant, h_words[quadrant][:].rearrange("p b x t -> p (b x t)"))

        def result_bank(job, t):
            gi, col0, width = job
            cols = slice(col0, col0 + width)
            if t == 0:
                y_f32[job] = new("y_f32_%d_%d" % (gi, col0), [P, SLOTS, width], F32)
            bank = psum.tile([P, HALF], F32, name="bank")
            terms = [(m, gj) for m in range(2) for gj in J_ORDER]
            for k, (m, gj) in enumerate(terms):
                h_codes, h_plane = h_mx[gi, m, gj]
                a_codes, a_plane = a_mx[m, gj]
                nc.tensor.matmul_mx(
                    out=bank[:, :width],
                    lhsT=h_codes[:, P * t : P * (t + 1)].bitcast(FP8X4), lhsT_scale=h_plane[:, P * t : P * (t + 1)],
                    rhs=a_codes[:, cols].bitcast(FP8X4), rhs_scale=a_plane[:, cols],
                    start=(k == 0), stop=(k == len(terms) - 1),
                )
            y = y_f32[job]
            nc.vector.scalar_tensor_tensor(
                out=y[:, t, :], in0=base_sb[gi][:, t, cols], scalar=lam_sb[:, gi, t : t + 1], in1=bank[:, :width],
                op0=ALU.mult, op1=ALU.add,
            )
            slots_per_store = N // width
            if (t + 1) % slots_per_store == 0:
                ts = slice(t + 1 - slots_per_store, t + 1)
                rows = out_0[HALF * gi : HALF * (gi + 1), cols].rearrange("(p t) n -> p t n", t=SLOTS)
                nc.sync.dma_start(out=rows[:, ts, :], in_=y[:, ts, :])

        def interleave_y(job, scalar_cols):
            gi, col0, width = job
            y = y_f32[job]
            y_words[job] = new("y_words_%d_%d" % (gi, col0), [P, width, SLOTS], BF16)
            if scalar_cols > 0:
                interleave(nc.scalar.copy, y_words[job][:, :scalar_cols, :], y[:, :, :scalar_cols])
            if scalar_cols < width:
                interleave(nc.vector.tensor_copy, y_words[job][:, scalar_cols:, :], y[:, :, scalar_cols:])

        def quantise_y(job):
            gi, col0, width = job
            cols = slice(col0, col0 + width)
            nc.vector.quantize_mx(
                out=y_codes[gi][:, cols].bitcast(FP8X4), scales=y_plane[4 * gi :, cols],
                in_=y_words[job][:].rearrange("p n t -> p (n t)"),
            )
            if (col0 + width) % WIDE == 0:
                done = slice(col0 + width - WIDE, col0 + width)
                words = out_1[gi].rearrange("p n t -> p (n t)").bitcast(I32)
                nc.sync.dma_start(out=words[:, done], in_=y_codes[gi][:, done].bitcast(I32))

        def store_y_plane():
            rows = out_2.rearrange("g (q r) n -> q g r n", r=4).bitcast(I32)
            for q in range(4):
                queue = nc.sync if q == 3 else nc.scalar
                queue.dma_start(out=rows[q], in_=y_plane[32 * q : 32 * q + 8, :].bitcast(I32))

        quadrants = [(gi, m, gj) for gi in range(2) for m in range(2) for gj in J_ORDER]
        s_copy, v_copy = nc.scalar.copy, nc.vector.tensor_copy

        def finish_quadrant(quadrant, unit):
            if unit == 0:
                join_pairs(quadrant, 1)
            if unit == 1:
                quantise_h(quadrant)

        def gram_step(index, beside, follows_quadrant=True):
            for unit in range(BANKS):
                gram_bank(quadrants[index], unit)
                if follows_quadrant:
                    finish_quadrant(quadrants[index - 1], unit)
                if unit == 2:
                    join_pairs(quadrants[index], 0)
                beside(unit)

        def result_step(job, quadrant_before=None):
            for t in range(BANKS):
                result_bank(job, t)
                if quadrant_before is not None:
                    finish_quadrant(quadrant_before, t)

        def sort_next_v(index):
            following = quadrants[index + 1]
            return lambda unit: sort_v(following[1], following[2]) if unit == 0 else None

        def beside_quadrant_3(unit):
            interleave_a(s_copy, 0, 1, unit, BANKS)
            if unit >= 2:
                interleave_a(v_copy, 0, 0, unit - 2, 2)

        def beside_quadrant_4(unit):
            interleave_a(s_copy, 1, 1, unit, BANKS)
            if unit >= 2:
                quantise_a(0, J_ORDER[unit - 2])

        def beside_quadrant_5(unit):
            if unit < 2:
                interleave_a(v_copy, 1, 0, unit, 2)
            if unit == 2:
                quantise_a(1, 1)

        def beside_quadrant_6(unit):
            if unit == 0:
                quantise_a(1, 0)

        jobs = [(0, 0, WIDE), (0, WIDE, WIDE), (1, 0, WIDE), (1, WIDE, NARROW), (1, WIDE + NARROW, NARROW)]

        def planes_of_first_job(unit):
            if unit == 0:
                interleave_y(jobs[0], 0)
            if unit == 1:
                quantise_y(jobs[0])

        sort_v(0, 1)
        gram_step(0, sort_next_v(0), follows_quadrant=False)
        gram_step(1, sort_next_v(1))
        gram_step(2, sort_next_v(2))
        gram_step(3, beside_quadrant_3)
        gram_step(4, beside_quadrant_4)
        gram_step(5, beside_quadrant_5)
        gram_step(6, beside_quadrant_6)
        result_step(jobs[0], quadrants[6])
        gram_step(7, planes_of_first_job, follows_quadrant=False)
        result_step(jobs[1], quadrants[7])
        interleave_y(jobs[1], WIDE)
        for k, scalar_cols in ((2, NARROW), (3, NARROW), (4, 0)):
            result_step(jobs[k])
            quantise_y(jobs[k - 1])
            interleave_y(jobs[k], scalar_cols)
        quantise_y(jobs[4])
        store_y_plane()
